import numpy as np
import ml_dtypes


def mxq(x, axis, fmt="e4m3"):
    dtype, down = {"e4m3": (ml_dtypes.float8_e4m3fn, 7), "e5m2": (ml_dtypes.float8_e5m2, 14)}[fmt]
    v = np.moveaxis(np.asarray(x, np.float32).astype(ml_dtypes.bfloat16).astype(np.float64), axis, -1)
    blocks = v.reshape(v.shape[:-1] + (-1, 32))
    amax = np.abs(blocks).max(-1, keepdims=True)
    byte = np.maximum(np.where(amax > 0, np.frexp(amax)[1] - 1 + 127, 0) - down, 1)
    scale = np.exp2(byte - 127.0)
    codes = (blocks / scale).astype(np.float32).astype(dtype).astype(np.float64)
    return np.moveaxis((codes * scale).reshape(v.shape), -1, axis)


WIDE = False


def mx_kscale(k):
    if not WIDE:
        return np.ones(k)
    levels = np.array([10, -10, 5, -5, 0])
    if k % 512:
        return np.exp2(np.random.permutation(np.resize(levels, k // 32))).repeat(32)
    a = np.empty((k // 512, 16))
    for p in range(k // 512):
        a[p, :8] = np.random.permutation(np.resize(levels, 8))
        for g in range(8):
            far = levels[np.abs(levels - a[p, g]) >= 10]
            a[p, g + 8] = far[np.random.randint(len(far))]
    return np.exp2(a.ravel()).repeat(32)


def f64(x):
    return np.asarray(x).astype(np.float64)


def striped(idx):
    return np.tile(idx.reshape(-1, 16).T, (8, 1)).astype(np.uint16)


def unstriped(offs):
    return offs[:16].T.reshape(-1).astype(np.int64)


E2M1 = np.array([0.0, 0.5, 1.0, 1.5, 2.0, 3.0, 4.0, 6.0, -0.0, -0.5, -1.0, -1.5, -2.0, -3.0, -4.0, -6.0])


def pack_weight(w, fmt):
    k, n = w.shape
    w = f64(np.asarray(w, np.float32).astype(ml_dtypes.bfloat16)).reshape(k // 32, 32, n)
    amax = np.abs(w).max(1)
    if fmt == "e4m3":
        byte = np.frexp(amax)[1] - 1 + 127 - 7
    else:
        mant, ex = np.frexp(amax / 6.0)
        byte = np.where(mant > 0.5, ex, ex - 1) + 127
    byte = np.clip(np.where(amax > 0, byte, 1), 1, 254)
    scaled = (w * np.exp2(127.0 - byte)[:, None, :]).reshape(k, n).astype(np.float32)
    by_word = np.ascontiguousarray(scaled.reshape(k // 512, 128, 4, n).transpose(0, 1, 3, 2))
    if fmt == "e4m3":
        words = by_word.astype(ml_dtypes.float8_e4m3fn).view(np.uint8)
    else:
        c = by_word.astype(ml_dtypes.float4_e2m1fn).view(np.uint8) & 0xF
        words = (c[..., 0::2] | (c[..., 1::2] << 4)).reshape(k // 512, 128, 2 * n)
    return np.ascontiguousarray(words), np.ascontiguousarray(byte.astype(np.uint8).reshape(k // 512, 16, n))


def unpack_weight(words, scales, fmt):
    g, _, n = scales.shape
    words = np.ascontiguousarray(words).reshape(g, 128, n, -1)
    if fmt == "e4m3":
        vals = words.view(ml_dtypes.float8_e4m3fn).astype(np.float64)
    else:
        nib = np.empty((g, 128, n, 4), np.uint8)
        nib[..., 0::2] = words & 0xF
        nib[..., 1::2] = words >> 4
        vals = E2M1[nib]
    vals = vals * np.repeat(np.exp2(scales.astype(np.float64) - 127.0), 8, axis=1)[..., None]
    return vals.transpose(0, 1, 3, 2).reshape(g * 512, n)


def gelu(v):
    return 0.5 * v * (1.0 + np.tanh(np.sqrt(2.0 / np.pi) * (v + 0.044715 * v**3)))


def striped8(idx):
    return np.concatenate([v.reshape(-1, 16).T for v in idx]).astype(np.uint16)


def unstriped8(offs):
    return np.stack([offs[16 * g:16 * g + 16].T.reshape(-1) for g in range(8)]).astype(np.int64)


def heads(h, wgt, idx8):
    r = np.arange(h.shape[0])
    return wgt[r // 4 % 128] * h[r[:, None], idx8[r % 512 // 64]]


def bf(x):
    return np.asarray(x, np.float32).astype(ml_dtypes.bfloat16)


def planes(Y):
    n, m = Y.shape
    b = f64(bf(Y)).reshape(n // 32, 32, m)
    amax = np.abs(b).max(1)
    byte = np.clip(np.where(amax > 0, np.frexp(amax)[1] - 1 + 127 - 7, 1), 1, 254)
    codes = (b * np.exp2(127.0 - byte)[:, None, :]).reshape(n, m).astype(np.float32).astype(ml_dtypes.float8_e4m3fn).view(np.uint8)
    words = codes.reshape(n // 512, 128, 4, m).transpose(0, 1, 3, 2)
    return np.ascontiguousarray(words), np.ascontiguousarray(byte.astype(np.uint8).reshape(n // 512, 16, m))


K, H, N, T, S, P = 1024, 1024, 512, 4096, 1024, 512

def setup_inputs():
    n = np.random.standard_normal
    s = mx_kscale(K)[:, None]
    u = mx_kscale(H)[:, None]
    tab_words, tab_scales = pack_weight(n((K, T)) * s, "e4m3")
    w1_words, w1_scales = pack_weight(0.6 * n((K, H)) / np.sqrt(K) / s * u.T, "e2m1")
    return {
        "tab_words": tab_words, "tab_scales": tab_scales,
        "offs": striped(np.random.permutation(T)[:S]),
        "w1_words": w1_words, "w1_scales": w1_scales,
        "wgt": np.repeat(np.random.uniform(0.5, 2.0, (8, P)), 16, axis=0).astype(np.float32),
        "offs2": striped8(np.stack([np.random.permutation(S)[:P] for _ in range(8)])),
        "a": (np.random.uniform(0.04, 0.12, H) / u[:, 0] ** 2).astype(np.float32),
        "w2": (n((H, N)) / np.sqrt(H) / u).astype(np.float32),
        "gain": np.exp(0.8 * n(N)).astype(np.float32),
    }

def reference(tab_words, tab_scales, offs, w1_words, w1_scales, wgt, offs2, a, w2, gain):
    v = unpack_weight(tab_words, tab_scales, "e4m3")[:, unstriped(offs)]
    w1 = unpack_weight(w1_words, w1_scales, "e2m1")
    h = w1.T @ v
    x = heads(h, f64(wgt), unstriped8(offs2))
    z = x - f64(a)[:, None] * x ** 3
    mix = mxq(f64(w2), 0, "e4m3").T @ mxq(z, 0, "e4m3")
    y = f64(gain)[:, None] * mix
    words, scales = planes(y)
    return y, words, scales

@@ -1,0 +1,277 @@
+from contextlib import ExitStack
+
+import concourse.mybir as mybir
+
+K, H, N, T, S, STEPS = 1024, 1024, 512, 4096, 1024, 512
+FLOPS = 2 * K * H * S + 2 * H * N * STEPS
+
+F32 = mybir.dt.float32
+BF16 = mybir.dt.bfloat16
+I32 = mybir.dt.int32
+U32 = mybir.dt.uint32
+U16 = mybir.dt.uint16
+U8 = mybir.dt.uint8
+FP8X4 = mybir.dt.float8_e4m3fn_x4
+FP4X4 = mybir.dt.float4_e2m1fn_x4
+MULT = mybir.AluOpType.mult
+ADD = mybir.AluOpType.add
+COPY = mybir.ActivationFunctionType.Copy
+SQUARE = mybir.ActivationFunctionType.Square
+
+P = 128
+PACK = 4
+BANK = 512
+HALF = STEPS // 2
+
+
+def tile_list_granular_waveshaper_kernel(
+    tc, tab_words, tab_scales, offs, w1_words, w1_scales, wgt, offs2, a, w2, gain, out_0, out_1, out_2
+):
+    nc = tc.nc
+    with ExitStack() as ctx:
+        keep = ctx.enter_context(tc.tile_pool(name="keep", bufs=1))
+        reuse = ctx.enter_context(tc.tile_pool(name="reuse", bufs=1))
+        ring = ctx.enter_context(tc.tile_pool(name="ring", bufs=4))
+        psum = ctx.enter_context(tc.psum_pool(name="psum", bufs=8))
+
+        list1 = keep.tile([P, S // 16], U16, name="list1")
+        list2 = keep.tile([P, STEPS // 16], U16, name="list2")
+        nc.sync.dma_start(list1[:], offs)
+        nc.sync.dma_start(list2[:], offs2)
+
+        scale_win = reuse.tile([P, T], U8, name="scale_win", tag="slot_a", align_bytes=64)
+        nc.vector.memset(scale_win[:].bitcast(I32), 0)
+        w1s_raw = reuse.tile([P, 2, H], U8, name="w1s_raw", tag="slot_c", align_bytes=64)
+        nc.gpsimd.memset(w1s_raw[:].rearrange("p a c -> p (a c)").bitcast(I32), 0)
+        plane1 = keep.tile([P, S], U8, name="plane1", align_bytes=64)
+        nc.vector.memset(plane1[:].bitcast(I32), 0)
+
+        w1_rows = w1_words.rearrange("a p c -> p a c")
+        w1_raw = [keep.tile([P, 2, H], U8, name="w1_raw%d" % b, align_bytes=64) for b in range(2)]
+        nc.sync.dma_start(w1_raw[0][:].bitcast(I32), w1_rows[:, :, 0:H].bitcast(I32))
+        table = []
+        for k in range(2):
+            words = reuse.tile([P, T], I32, name="table%d" % k, tag="slot_t%d" % k, align_bytes=64)
+            nc.sync.dma_start(words[:], tab_words[k].rearrange("p n t -> p (n t)").bitcast(I32))
+            table.append(words)
+        nc.sync.dma_start(w1_raw[1][:].bitcast(I32), w1_rows[:, :, H : 2 * H].bitcast(I32))
+        for q in range(4):
+            nc.scalar.dma_start(
+                scale_win[32 * q : 32 * q + 8, :].bitcast(I32), tab_scales[:, 4 * q : 4 * q + 4, :].bitcast(I32)
+            )
+        for q in range(4):
+            nc.gpsimd.dma_start(
+                w1s_raw[32 * q : 32 * q + 4, :, :].bitcast(I32),
+                w1_scales[:, 4 * q : 4 * q + 4, :].rearrange("a r c -> r a c").bitcast(I32),
+            )
+        coef = keep.tile([P, 2, PACK], F32, name="coef")
+        nc.scalar.dma_start(coef[:], a.rearrange("(b p i) -> p b i", b=2, i=PACK))
+        neg_coef = keep.tile([P, 2, PACK], F32, name="neg_coef")
+        nc.scalar.activation(neg_coef[:], coef[:], COPY, scale=-1.0)
+
+        plane0 = keep.tile([P, S], U8, name="plane0", align_bytes=64)
+        nc.vector.tensor_copy(plane0[:], scale_win[:].indirect(list1[:]))
+        nc.scalar.dma_start(plane1[0:100, :].bitcast(I32), plane0[4:104, :].bitcast(I32))
+        planes = [plane0, plane1]
+
+        w1_s = keep.tile([P, 2, H], U8, name="w1_s", align_bytes=64)
+        nc.vector.tensor_copy(
+            w1_s[:].rearrange("p a (b i m) -> p (a b) i m", b=2, i=PACK),
+            w1s_raw[:].rearrange("p a (b m i) -> p (a b) i m", b=2, i=PACK),
+        )
+
+        def deal_w1(b):
+            dealt = keep.tile([P, 2, H], U8, name="w1_q%d" % b, align_bytes=64)
+            nc.vector.tensor_copy(
+                dealt[:].bitcast(U16).rearrange("p a (i m) -> p a i m", i=PACK),
+                w1_raw[b][:].bitcast(U16).rearrange("p a (m i) -> p a i m", i=PACK),
+            )
+            return dealt
+
+        w1_q = [deal_w1(0)]
+
+        gains = reuse.tile([P, PACK], F32, name="gains", tag="slot_c", align_bytes=64)
+        nc.gpsimd.dma_start(gains[:], gain.rearrange("(p t) -> p t", t=PACK))
+        env = reuse.tile([P, STEPS], F32, name="env", tag="slot_a", align_bytes=64)
+        nc.sync.dma_start(env[:], wgt)
+
+        picked = [[None, None], [None, None]]
+        for k in range(2):
+            for s in range(2):
+                g = keep.tile([P, BANK], U32, name="picked%d%d" % (k, s), align_bytes=64)
+                nc.vector.tensor_copy(g[:], table[k][:].bitcast(U32).indirect(list1[:, 32 * s : 32 * (s + 1)]))
+                picked[k][s] = g
+
+        w1_q.append(deal_w1(1))
+        w2_raw = reuse.tile([P, 2, PACK * N], F32, name="w2_raw", tag="slot_t0", align_bytes=64)
+        for b in range(2):
+            nc.sync.dma_start(
+                w2_raw[:, b, :], w2[512 * b : 512 * (b + 1), :].rearrange("(p j) n -> p (j n)", j=PACK)
+            )
+
+        def make_h(b, i):
+            rows = keep.tile([P, S], F32, name="h%d%d" % (b, i), align_bytes=64)
+            c0 = 512 * b + P * i
+            for s in range(2):
+                acc = psum.tile([P, BANK], F32, name="acc", tag="bank")
+                for k in range(2):
+                    nc.tensor.matmul_mx(
+                        out=acc[:],
+                        lhsT=w1_q[b][:, k, 2 * P * i : 2 * P * (i + 1)].bitcast(FP4X4),
+                        lhsT_scale=w1_s[:, k, c0 : c0 + P],
+                        rhs=picked[k][s][:].bitcast(FP8X4),
+                        rhs_scale=planes[k][:, BANK * s : BANK * (s + 1)],
+                        start=(k == 0),
+                        stop=(k == 1),
+                    )
+                nc.scalar.activation(rows[:, BANK * s : BANK * (s + 1)], acc[:], COPY)
+            return rows
+
+        def chunk_tiles(b, m0, width):
+            x = keep.tile([P, PACK, width], F32, name="x%d_%d" % (b, m0), align_bytes=64)
+            u = keep.tile([P, PACK, width], F32, name="u%d_%d" % (b, m0), align_bytes=64)
+            return b, m0, width, x, u
+
+        def pick(chunk, i):
+            b, m0, width, x, u = chunk
+            nc.vector.tensor_tensor(
+                x[:, i, :],
+                h[b][i][:].indirect(list2[:, m0 // 16 : (m0 + width) // 16]),
+                env[:, m0 : m0 + width],
+                MULT,
+            )
+
+        def factor(chunk, i, on_vector=False):
+            b, m0, width, x, u = chunk
+            sq = ring.tile([P, width], F32, name="sq", tag="sq")
+            nc.scalar.activation(sq[:], x[:, i, :], SQUARE)
+            if on_vector:
+                nc.vector.tensor_scalar(u[:, i, :], sq[:], neg_coef[:, b, i : i + 1], 1.0, MULT, ADD)
+            else:
+                nc.scalar.activation(u[:, i, :], sq[:], COPY, bias=1.0, scale=neg_coef[:, b, i : i + 1])
+
+        def shape(chunk):
+            b, m0, width, x, u = chunk
+            z = keep.tile([P, width, PACK], BF16, name="z%d_%d" % (b, m0), align_bytes=64)
+            nc.vector.tensor_tensor(
+                z[:].rearrange("p (c e) i -> p c i e", e=4),
+                x[:].rearrange("p i (c e) -> p c i e", e=4),
+                u[:].rearrange("p i (c e) -> p c i e", e=4),
+                MULT,
+            )
+            return z
+
+        def quantise(name, grouped, width):
+            codes = keep.tile([P, width], U32, name=name + "_q", align_bytes=64)
+            scales = keep.tile([P, width], U8, name=name + "_s", align_bytes=64)
+            nc.vector.quantize_mx(codes[:].bitcast(FP8X4), scales[:], grouped)
+            return codes, scales
+
+        def round_w2(b, part):
+            ms = slice(64 * part, 64 * (part + 1))
+            nc.scalar.activation(
+                w2_bf[b][:].rearrange("p t m j -> p m j t")[:, ms],
+                w2_raw[:, b, :].rearrange("p (j m t) -> p m j t", j=PACK, t=PACK)[:, ms],
+                COPY,
+            )
+
+        y_scales = keep.tile([P, STEPS], U8, name="y_scales", align_bytes=64)
+        y_rows = out_0.rearrange("(p t) m -> p t m", t=PACK)
+        y_words = out_1[0].rearrange("p m t -> p (m t)").bitcast(I32)
+
+        def mix(s, z1, share):
+            m0 = HALF * s
+            y = keep.tile([P, PACK, HALF], F32, name="y%d" % s, align_bytes=64)
+            for t in range(PACK):
+                acc = psum.tile([P, HALF], F32, name="mix", tag="bank")
+                for b in range(2):
+                    z_q, z_s = (z0, z1)[b]
+                    cols = slice(m0, m0 + HALF) if b == 0 else slice(0, HALF)
+                    nc.tensor.matmul_mx(
+                        out=acc[:],
+                        lhsT=w2_q[b][0][:, P * t : P * (t + 1)].bitcast(FP8X4),
+                        lhsT_scale=w2_q[b][1][:, P * t : P * (t + 1)],
+                        rhs=z_q[:, cols].bitcast(FP8X4),
+                        rhs_scale=z_s[:, cols],
+                        start=(b == 0),
+                        stop=(b == 1),
+                    )
+                if share and t % 2:
+                    nc.vector.tensor_scalar(y[:, t, :], acc[:], gains[:, t : t + 1], None, MULT)
+                else:
+                    nc.scalar.activation(y[:, t, :], acc[:], COPY, scale=gains[:, t : t + 1])
+            nc.sync.dma_start(y_rows[:, :, m0 : m0 + HALF], y[:])
+            return y
+
+        def round_y(s, y):
+            y_bf = keep.tile([P, HALF, PACK], BF16, name="y_bf%d" % s, align_bytes=64)
+            nc.vector.tensor_copy(
+                y_bf[:].rearrange("p (c e) t -> p c t e", e=4), y[:].rearrange("p t (c e) -> p c t e", e=4)
+            )
+            return y_bf
+
+        def planes_out(s, y_bf):
+            m0 = HALF * s
+            y_q = keep.tile([P, HALF], U32, name="y_q%d" % s, align_bytes=64)
+            nc.vector.quantize_mx(
+                y_q[:].bitcast(FP8X4), y_scales[:, m0 : m0 + HALF], y_bf[:].rearrange("p m t -> p (m t)")
+            )
+            nc.sync.dma_start(y_words[:, m0 : m0 + HALF], y_q[:].bitcast(I32))
+
+        flat = "p m i -> p (m i)"
+        h = [[], []]
+        w2_bf = [keep.tile([P, PACK, P, PACK], BF16, name="w2_bf%d" % b, align_bytes=64) for b in range(2)]
+        c0 = chunk_tiles(0, 0, STEPS)
+        c1 = [chunk_tiles(1, HALF * s, HALF) for s in range(2)]
+        h[0].append(make_h(0, 0))
+        pick(c0, 0)
+        h[0].append(make_h(0, 1))
+        pick(c0, 1)
+        h[0].append(make_h(0, 2))
+        factor(c0, 0, True)
+        pick(c0, 2)
+        h[0].append(make_h(0, 3))
+        factor(c0, 1, True)
+        pick(c0, 3)
+        h[1].append(make_h(1, 0))
+        factor(c0, 2, True)
+        pick(c1[0], 0)
+        h[1].append(make_h(1, 1))
+        factor(c0, 3)
+        pick(c1[0], 1)
+        h[1].append(make_h(1, 2))
+        zb0 = shape(c0)
+        h[1].append(make_h(1, 3))
+        pick(c1[0], 2)
+        z0 = quantise("z0", zb0[:].rearrange(flat), STEPS)
+        factor(c1[0], 0)
+        factor(c1[0], 1)
+        pick(c1[0], 3)
+        factor(c1[0], 2)
+        factor(c1[0], 3)
+        round_w2(0, 0)
+        round_w2(0, 1)
+        pick(c1[1], 0)
+        pick(c1[1], 1)
+        zb1 = shape(c1[0])
+        round_w2(1, 0)
+        round_w2(1, 1)
+        w2_q = [quantise("w2_0", w2_bf[0][:].rearrange("p t m j -> p (t m j)"), N)]
+        pick(c1[1], 2)
+        z1 = quantise("z1_0", zb1[:].rearrange(flat), HALF)
+        pick(c1[1], 3)
+        w2_q.append(quantise("w2_1", w2_bf[1][:].rearrange("p t m j -> p (t m j)"), N))
+        for i in range(PACK):
+            factor(c1[1], i)
+        y0 = mix(0, z1, False)
+        zb1 = shape(c1[1])
+        yb0 = round_y(0, y0)
+        z1 = quantise("z1_1", zb1[:].rearrange(flat), HALF)
+        planes_out(0, yb0)
+        y1 = mix(1, z1, True)
+        planes_out(1, round_y(1, y1))
+        for q in range(4):
+            engine = nc.scalar if q % 2 else nc.sync
+            engine.dma_start(
+                out_2[0, 4 * q : 4 * q + 4, :].bitcast(I32), y_scales[32 * q : 32 * q + 4, :].bitcast(I32)
+            )

@@ -36,49 +36,55 @@ def tile_list_granular_waveshaper_kernel(
 
         list1 = keep.tile([P, S // 16], U16, name="list1")
         list2 = keep.tile([P, STEPS // 16], U16, name="list2")
-        nc.sync.dma_start(list1[:], offs)
-        nc.sync.dma_start(list2[:], offs2)
-
         scale_win = reuse.tile([P, T], U8, name="scale_win", tag="slot_a", align_bytes=64)
-        nc.vector.memset(scale_win[:].bitcast(I32), 0)
-        w1s_raw = reuse.tile([P, 2, H], U8, name="w1s_raw", tag="slot_c", align_bytes=64)
+        w1s_raw = reuse.tile([P, 2, H], U8, name="w1s_raw", tag="slot_b", align_bytes=64)
+        planes = [keep.tile([P, S], U8, name="plane%d" % k, align_bytes=64) for k in range(2)]
         nc.gpsimd.memset(w1s_raw[:].rearrange("p a c -> p (a c)").bitcast(I32), 0)
-        plane1 = keep.tile([P, S], U8, name="plane1", align_bytes=64)
-        nc.vector.memset(plane1[:].bitcast(I32), 0)
+        for q in range(4):
+            nc.vector.memset(scale_win[32 * q : 32 * q + 24, :].bitcast(I32), 0)
+        for k in range(2):
+            nc.gpsimd.memset(planes[k][96:P, :].bitcast(I32), 0)
 
         w1_rows = w1_words.rearrange("a p c -> p a c")
-        w1_raw = [keep.tile([P, 2, H], U8, name="w1_raw%d" % b, align_bytes=64) for b in range(2)]
-        nc.sync.dma_start(w1_raw[0][:].bitcast(I32), w1_rows[:, :, 0:H].bitcast(I32))
-        table = []
-        for k in range(2):
-            words = reuse.tile([P, T], I32, name="table%d" % k, tag="slot_t%d" % k, align_bytes=64)
-            nc.sync.dma_start(words[:], tab_words[k].rearrange("p n t -> p (n t)").bitcast(I32))
-            table.append(words)
-        nc.sync.dma_start(w1_raw[1][:].bitcast(I32), w1_rows[:, :, H : 2 * H].bitcast(I32))
+        w1_raw = [keep.tile([P, 2, H], U8, name="w1_raw0", align_bytes=64)]
+        table = [reuse.tile([P, T], I32, name="table%d" % k, tag="slot_t%d" % k, align_bytes=64) for k in range(2)]
+        coef = keep.tile([P, 2, PACK], F32, name="coef")
+
+        nc.sync.dma_start(list1[:], offs)
         for q in range(4):
-            nc.scalar.dma_start(
-                scale_win[32 * q : 32 * q + 8, :].bitcast(I32), tab_scales[:, 4 * q : 4 * q + 4, :].bitcast(I32)
+            nc.sync.dma_start(
+                scale_win[32 * q + 24 : 32 * q + 32, :].bitcast(I32), tab_scales[:, 4 * q : 4 * q + 4, :].bitcast(I32)
             )
+        nc.sync.dma_start(list2[:], offs2)
+        nc.sync.dma_start(w1_raw[0][:].bitcast(I32), w1_rows[:, :, 0:H].bitcast(I32))
+        nc.sync.dma_start(table[0][:], tab_words[0].rearrange("p n t -> p (n t)").bitcast(I32))
         for q in range(4):
-            nc.gpsimd.dma_start(
+            nc.sync.dma_start(
                 w1s_raw[32 * q : 32 * q + 4, :, :].bitcast(I32),
                 w1_scales[:, 4 * q : 4 * q + 4, :].rearrange("a r c -> r a c").bitcast(I32),
             )
-        coef = keep.tile([P, 2, PACK], F32, name="coef")
-        nc.scalar.dma_start(coef[:], a.rearrange("(b p i) -> p b i", b=2, i=PACK))
+        nc.sync.dma_start(coef[:], a.rearrange("(b p i) -> p b i", b=2, i=PACK))
+        nc.sync.dma_start(table[1][:], tab_words[1].rearrange("p n t -> p (n t)").bitcast(I32))
+
         neg_coef = keep.tile([P, 2, PACK], F32, name="neg_coef")
         nc.scalar.activation(neg_coef[:], coef[:], COPY, scale=-1.0)
 
-        plane0 = keep.tile([P, S], U8, name="plane0", align_bytes=64)
-        nc.vector.tensor_copy(plane0[:], scale_win[:].indirect(list1[:]))
-        nc.scalar.dma_start(plane1[0:100, :].bitcast(I32), plane0[4:104, :].bitcast(I32))
-        planes = [plane0, plane1]
+        scale_rows = keep.tile([P, S], U8, name="scale_rows", align_bytes=64)
+        nc.vector.tensor_copy(scale_rows[:], scale_win[:].indirect(list1[:]))
+        for k in range(2):
+            nc.scalar.dma_start(
+                planes[k][0:100, :].bitcast(I32), scale_rows[24 + 4 * k : 124 + 4 * k, :].bitcast(I32)
+            )
+        w1_raw.append(reuse.tile([P, 2, H], U8, name="w1_raw1", tag="slot_a", align_bytes=64))
+        nc.sync.dma_start(w1_raw[1][:].bitcast(I32), w1_rows[:, :, H : 2 * H].bitcast(I32))
 
         w1_s = keep.tile([P, 2, H], U8, name="w1_s", align_bytes=64)
         nc.vector.tensor_copy(
             w1_s[:].rearrange("p a (b i m) -> p (a b) i m", b=2, i=PACK),
             w1s_raw[:].rearrange("p a (b m i) -> p (a b) i m", b=2, i=PACK),
         )
+        env = reuse.tile([P, STEPS], F32, name="env", tag="slot_b", align_bytes=64)
+        nc.sync.dma_start(env[:], wgt)
 
         def deal_w1(b):
             dealt = keep.tile([P, 2, H], U8, name="w1_q%d" % b, align_bytes=64)
@@ -89,41 +95,48 @@ def tile_list_granular_waveshaper_kernel(
             return dealt
 
         w1_q = [deal_w1(0)]
-
-        gains = reuse.tile([P, PACK], F32, name="gains", tag="slot_c", align_bytes=64)
-        nc.gpsimd.dma_start(gains[:], gain.rearrange("(p t) -> p t", t=PACK))
-        env = reuse.tile([P, STEPS], F32, name="env", tag="slot_a", align_bytes=64)
-        nc.sync.dma_start(env[:], wgt)
-
         picked = [[None, None], [None, None]]
         for k in range(2):
             for s in range(2):
                 g = keep.tile([P, BANK], U32, name="picked%d%d" % (k, s), align_bytes=64)
                 nc.vector.tensor_copy(g[:], table[k][:].bitcast(U32).indirect(list1[:, 32 * s : 32 * (s + 1)]))
                 picked[k][s] = g
-
         w1_q.append(deal_w1(1))
         w2_raw = reuse.tile([P, 2, PACK * N], F32, name="w2_raw", tag="slot_t0", align_bytes=64)
         for b in range(2):
             nc.sync.dma_start(
                 w2_raw[:, b, :], w2[512 * b : 512 * (b + 1), :].rearrange("(p j) n -> p (j n)", j=PACK)
             )
+        gains = reuse.tile([P, PACK], F32, name="gains", tag="slot_a", align_bytes=64)
+        nc.sync.dma_start(gains[:], gain.rearrange("(p t) -> p t", t=PACK))
+
+        def first_product(acc, b, i, s, k):
+            c0 = 512 * b + P * i
+            nc.tensor.matmul_mx(
+                out=acc[:],
+                lhsT=w1_q[b][:, k, 2 * P * i : 2 * P * (i + 1)].bitcast(FP4X4),
+                lhsT_scale=w1_s[:, k, c0 : c0 + P],
+                rhs=picked[k][s][:].bitcast(FP8X4),
+                rhs_scale=planes[k][:, BANK * s : BANK * (s + 1)],
+                start=(k == 0),
+                stop=(k == 1),
+            )
+
+        opened = {}
+        for s in range(2):
+            for i in range(PACK):
+                opened[i, s] = psum.tile([P, BANK], F32, name="acc", tag="bank")
+                first_product(opened[i, s], 0, i, s, 0)
 
         def make_h(b, i):
-            rows = keep.tile([P, S], F32, name="h%d%d" % (b, i), align_bytes=64)
-            c0 = 512 * b + P * i
+            rows = reuse.tile([P, S], F32, name="h%d%d" % (b, i), tag="h%d%d" % (b, i), align_bytes=64)
             for s in range(2):
-                acc = psum.tile([P, BANK], F32, name="acc", tag="bank")
-                for k in range(2):
-                    nc.tensor.matmul_mx(
-                        out=acc[:],
-                        lhsT=w1_q[b][:, k, 2 * P * i : 2 * P * (i + 1)].bitcast(FP4X4),
-                        lhsT_scale=w1_s[:, k, c0 : c0 + P],
-                        rhs=picked[k][s][:].bitcast(FP8X4),
-                        rhs_scale=planes[k][:, BANK * s : BANK * (s + 1)],
-                        start=(k == 0),
-                        stop=(k == 1),
-                    )
+                if b == 0:
+                    acc = opened[i, s]
+                else:
+                    acc = psum.tile([P, BANK], F32, name="acc", tag="bank")
+                    first_product(acc, b, i, s, 0)
+                first_product(acc, b, i, s, 1)
                 nc.scalar.activation(rows[:, BANK * s : BANK * (s + 1)], acc[:], COPY)
             return rows
 
@@ -220,7 +233,7 @@ def tile_list_granular_waveshaper_kernel(
 
         flat = "p m i -> p (m i)"
         h = [[], []]
-        w2_bf = [keep.tile([P, PACK, P, PACK], BF16, name="w2_bf%d" % b, align_bytes=64) for b in range(2)]
+        w2_bf = []
         c0 = chunk_tiles(0, 0, STEPS)
         c1 = [chunk_tiles(1, HALF * s, HALF) for s in range(2)]
         h[0].append(make_h(0, 0))
@@ -237,32 +250,32 @@ def tile_list_granular_waveshaper_kernel(
         factor(c0, 2, True)
         pick(c1[0], 0)
         h[1].append(make_h(1, 1))
-        factor(c0, 3)
+        factor(c0, 3, True)
         pick(c1[0], 1)
         h[1].append(make_h(1, 2))
+        pick(c1[1], 0)
         zb0 = shape(c0)
         h[1].append(make_h(1, 3))
         pick(c1[0], 2)
         z0 = quantise("z0", zb0[:].rearrange(flat), STEPS)
-        factor(c1[0], 0)
-        factor(c1[0], 1)
-        pick(c1[0], 3)
-        factor(c1[0], 2)
-        factor(c1[0], 3)
+        w2_bf.append(reuse.tile([P, PACK, P, PACK], BF16, name="w2_bf0", tag="h02", align_bytes=64))
         round_w2(0, 0)
         round_w2(0, 1)
-        pick(c1[1], 0)
+        pick(c1[0], 3)
+        for i in range(PACK):
+            factor(c1[0], i)
         pick(c1[1], 1)
-        zb1 = shape(c1[0])
+        w2_q = [quantise("w2_0", w2_bf[0][:].rearrange("p t m j -> p (t m j)"), N)]
+        w2_bf.append(reuse.tile([P, PACK, P, PACK], BF16, name="w2_bf1", tag="h03", align_bytes=64))
         round_w2(1, 0)
         round_w2(1, 1)
-        w2_q = [quantise("w2_0", w2_bf[0][:].rearrange("p t m j -> p (t m j)"), N)]
         pick(c1[1], 2)
-        z1 = quantise("z1_0", zb1[:].rearrange(flat), HALF)
+        zb1 = shape(c1[0])
         pick(c1[1], 3)
+        z1 = quantise("z1_0", zb1[:].rearrange(flat), HALF)
         w2_q.append(quantise("w2_1", w2_bf[1][:].rearrange("p t m j -> p (t m j)"), N))
         for i in range(PACK):
-            factor(c1[1], i)
+            factor(c1[1], i, True)
         y0 = mix(0, z1, False)
         zb1 = shape(c1[1])
         yb0 = round_y(0, y0)

@@ -40,21 +40,18 @@ def tile_list_granular_waveshaper_kernel(
         w1s_raw = reuse.tile([P, 2, H], U8, name="w1s_raw", tag="slot_b", align_bytes=64)
         planes = [keep.tile([P, S], U8, name="plane%d" % k, align_bytes=64) for k in range(2)]
         nc.gpsimd.memset(w1s_raw[:].rearrange("p a c -> p (a c)").bitcast(I32), 0)
-        for q in range(4):
-            nc.vector.memset(scale_win[32 * q : 32 * q + 24, :].bitcast(I32), 0)
+        nc.vector.memset(scale_win[32:64, :].bitcast(I32), 0)
+        nc.vector.memset(scale_win[64:P, :].bitcast(I32), 0)
         for k in range(2):
-            nc.gpsimd.memset(planes[k][96:P, :].bitcast(I32), 0)
+            nc.gpsimd.memset(planes[k][:].bitcast(I32), 0)
 
         w1_rows = w1_words.rearrange("a p c -> p a c")
-        w1_raw = [keep.tile([P, 2, H], U8, name="w1_raw0", align_bytes=64)]
+        w1_raw = [reuse.tile([P, 2, H], U8, name="w1_raw0", tag="slot_w", align_bytes=64)]
         table = [reuse.tile([P, T], I32, name="table%d" % k, tag="slot_t%d" % k, align_bytes=64) for k in range(2)]
         coef = keep.tile([P, 2, PACK], F32, name="coef")
 
         nc.sync.dma_start(list1[:], offs)
-        for q in range(4):
-            nc.sync.dma_start(
-                scale_win[32 * q + 24 : 32 * q + 32, :].bitcast(I32), tab_scales[:, 4 * q : 4 * q + 4, :].bitcast(I32)
-            )
+        nc.sync.dma_start(scale_win[0:32, :].bitcast(I32), tab_scales.rearrange("a q t -> (a q) t").bitcast(I32))
         nc.sync.dma_start(list2[:], offs2)
         nc.sync.dma_start(w1_raw[0][:].bitcast(I32), w1_rows[:, :, 0:H].bitcast(I32))
         nc.sync.dma_start(table[0][:], tab_words[0].rearrange("p n t -> p (n t)").bitcast(I32))
@@ -72,9 +69,12 @@ def tile_list_granular_waveshaper_kernel(
         scale_rows = keep.tile([P, S], U8, name="scale_rows", align_bytes=64)
         nc.vector.tensor_copy(scale_rows[:], scale_win[:].indirect(list1[:]))
         for k in range(2):
-            nc.scalar.dma_start(
-                planes[k][0:100, :].bitcast(I32), scale_rows[24 + 4 * k : 124 + 4 * k, :].bitcast(I32)
-            )
+            for q in range(4):
+                engine = nc.gpsimd if k == 1 and q > 0 else nc.scalar
+                row = 16 * k + 4 * q
+                engine.dma_start(
+                    planes[k][32 * q : 32 * q + 4, :].bitcast(I32), scale_rows[row : row + 4, :].bitcast(I32)
+                )
         w1_raw.append(reuse.tile([P, 2, H], U8, name="w1_raw1", tag="slot_a", align_bytes=64))
         nc.sync.dma_start(w1_raw[1][:].bitcast(I32), w1_rows[:, :, H : 2 * H].bitcast(I32))
 
@@ -83,8 +83,6 @@ def tile_list_granular_waveshaper_kernel(
             w1_s[:].rearrange("p a (b i m) -> p (a b) i m", b=2, i=PACK),
             w1s_raw[:].rearrange("p a (b m i) -> p (a b) i m", b=2, i=PACK),
         )
-        env = reuse.tile([P, STEPS], F32, name="env", tag="slot_b", align_bytes=64)
-        nc.sync.dma_start(env[:], wgt)
 
         def deal_w1(b):
             dealt = keep.tile([P, 2, H], U8, name="w1_q%d" % b, align_bytes=64)
@@ -95,6 +93,8 @@ def tile_list_granular_waveshaper_kernel(
             return dealt
 
         w1_q = [deal_w1(0)]
+        env = reuse.tile([P, STEPS], F32, name="env", tag="slot_w", align_bytes=64)
+        nc.sync.dma_start(env[:], wgt)
         picked = [[None, None], [None, None]]
         for k in range(2):
             for s in range(2):
@@ -154,22 +154,25 @@ def tile_list_granular_waveshaper_kernel(
                 MULT,
             )
 
-        def factor(chunk, i, on_vector=False):
+        def factor(chunk, first, count, on_vector):
             b, m0, width, x, u = chunk
-            sq = ring.tile([P, width], F32, name="sq", tag="sq")
-            nc.scalar.activation(sq[:], x[:, i, :], SQUARE)
-            if on_vector:
-                nc.vector.tensor_scalar(u[:, i, :], sq[:], neg_coef[:, b, i : i + 1], 1.0, MULT, ADD)
-            else:
-                nc.scalar.activation(u[:, i, :], sq[:], COPY, bias=1.0, scale=neg_coef[:, b, i : i + 1])
+            sq = ring.tile([P, count, width], F32, name="sq", tag="sq")
+            nc.scalar.activation(sq[:], x[:, first : first + count, :], SQUARE)
+            for i in range(first, first + count):
+                if on_vector:
+                    nc.vector.tensor_scalar(u[:, i, :], sq[:, i - first, :], neg_coef[:, b, i : i + 1], 1.0, MULT, ADD)
+                else:
+                    nc.scalar.activation(
+                        u[:, i, :], sq[:, i - first, :], COPY, bias=1.0, scale=neg_coef[:, b, i : i + 1]
+                    )
 
         def shape(chunk):
             b, m0, width, x, u = chunk
             z = keep.tile([P, width, PACK], BF16, name="z%d_%d" % (b, m0), align_bytes=64)
             nc.vector.tensor_tensor(
-                z[:].rearrange("p (c e) i -> p c i e", e=4),
-                x[:].rearrange("p i (c e) -> p c i e", e=4),
-                u[:].rearrange("p i (c e) -> p c i e", e=4),
+                z[:].rearrange("p (c e) i -> p c i e", e=2),
+                x[:].rearrange("p i (c e) -> p c i e", e=2),
+                u[:].rearrange("p i (c e) -> p c i e", e=2),
                 MULT,
             )
             return z
@@ -180,11 +183,11 @@ def tile_list_granular_waveshaper_kernel(
             nc.vector.quantize_mx(codes[:].bitcast(FP8X4), scales[:], grouped)
             return codes, scales
 
-        def round_w2(b, part):
-            ms = slice(64 * part, 64 * (part + 1))
+        def round_w2(b, pair):
+            ts = slice(2 * pair, 2 * pair + 2)
             nc.scalar.activation(
-                w2_bf[b][:].rearrange("p t m j -> p m j t")[:, ms],
-                w2_raw[:, b, :].rearrange("p (j m t) -> p m j t", j=PACK, t=PACK)[:, ms],
+                w2_bf[b][:, ts].rearrange("p t m j -> p m j t"),
+                w2_raw[:, b, :].rearrange("p (j m t) -> p m j t", j=PACK, t=PACK)[:, :, :, ts],
                 COPY,
             )
 
@@ -219,7 +222,7 @@ def tile_list_granular_waveshaper_kernel(
         def round_y(s, y):
             y_bf = keep.tile([P, HALF, PACK], BF16, name="y_bf%d" % s, align_bytes=64)
             nc.vector.tensor_copy(
-                y_bf[:].rearrange("p (c e) t -> p c t e", e=4), y[:].rearrange("p t (c e) -> p c t e", e=4)
+                y_bf[:].rearrange("p (c e) t -> p c t e", e=2), y[:].rearrange("p t (c e) -> p c t e", e=2)
             )
             return y_bf
 
@@ -241,16 +244,16 @@ def tile_list_granular_waveshaper_kernel(
         h[0].append(make_h(0, 1))
         pick(c0, 1)
         h[0].append(make_h(0, 2))
-        factor(c0, 0, True)
+        factor(c0, 0, 1, True)
         pick(c0, 2)
         h[0].append(make_h(0, 3))
-        factor(c0, 1, True)
+        factor(c0, 1, 1, True)
         pick(c0, 3)
         h[1].append(make_h(1, 0))
-        factor(c0, 2, True)
+        factor(c0, 2, 1, True)
         pick(c1[0], 0)
         h[1].append(make_h(1, 1))
-        factor(c0, 3, True)
+        factor(c0, 3, 1, True)
         pick(c1[0], 1)
         h[1].append(make_h(1, 2))
         pick(c1[1], 0)
@@ -262,8 +265,8 @@ def tile_list_granular_waveshaper_kernel(
         round_w2(0, 0)
         round_w2(0, 1)
         pick(c1[0], 3)
-        for i in range(PACK):
-            factor(c1[0], i)
+        factor(c1[0], 0, 2, False)
+        factor(c1[0], 2, 2, False)
         pick(c1[1], 1)
         w2_q = [quantise("w2_0", w2_bf[0][:].rearrange("p t m j -> p (t m j)"), N)]
         w2_bf.append(reuse.tile([P, PACK, P, PACK], BF16, name="w2_bf1", tag="h03", align_bytes=64))
@@ -274,8 +277,8 @@ def tile_list_granular_waveshaper_kernel(
         pick(c1[1], 3)
         z1 = quantise("z1_0", zb1[:].rearrange(flat), HALF)
         w2_q.append(quantise("w2_1", w2_bf[1][:].rearrange("p t m j -> p (t m j)"), N))
-        for i in range(PACK):
-            factor(c1[1], i, True)
+        factor(c1[1], 0, 2, False)
+        factor(c1[1], 2, 2, True)
         y0 = mix(0, z1, False)
         zb1 = shape(c1[1])
         yb0 = round_y(0, y0)

@@ -40,43 +40,39 @@ def tile_list_granular_waveshaper_kernel(
         w1s_raw = reuse.tile([P, 2, H], U8, name="w1s_raw", tag="slot_b", align_bytes=64)
         planes = [keep.tile([P, S], U8, name="plane%d" % k, align_bytes=64) for k in range(2)]
         nc.gpsimd.memset(w1s_raw[:].rearrange("p a c -> p (a c)").bitcast(I32), 0)
-        nc.vector.memset(scale_win[32:64, :].bitcast(I32), 0)
-        nc.vector.memset(scale_win[64:P, :].bitcast(I32), 0)
+        nc.vector.memset(scale_win[0:96, :].bitcast(I32), 0)
         for k in range(2):
             nc.gpsimd.memset(planes[k][:].bitcast(I32), 0)
 
         w1_rows = w1_words.rearrange("a p c -> p a c")
         w1_raw = [reuse.tile([P, 2, H], U8, name="w1_raw0", tag="slot_w", align_bytes=64)]
-        table = [reuse.tile([P, T], I32, name="table%d" % k, tag="slot_t%d" % k, align_bytes=64) for k in range(2)]
-        coef = keep.tile([P, 2, PACK], F32, name="coef")
+        table = [reuse.tile([P, T], I32, name="table0", tag="slot_t0", align_bytes=64)]
 
         nc.sync.dma_start(list1[:], offs)
-        nc.sync.dma_start(scale_win[0:32, :].bitcast(I32), tab_scales.rearrange("a q t -> (a q) t").bitcast(I32))
-        nc.sync.dma_start(list2[:], offs2)
+        nc.sync.dma_start(scale_win[96:P, :].bitcast(I32), tab_scales.rearrange("a q t -> (a q) t").bitcast(I32))
         nc.sync.dma_start(w1_raw[0][:].bitcast(I32), w1_rows[:, :, 0:H].bitcast(I32))
-        nc.sync.dma_start(table[0][:], tab_words[0].rearrange("p n t -> p (n t)").bitcast(I32))
         for q in range(4):
             nc.sync.dma_start(
                 w1s_raw[32 * q : 32 * q + 4, :, :].bitcast(I32),
                 w1_scales[:, 4 * q : 4 * q + 4, :].rearrange("a r c -> r a c").bitcast(I32),
             )
-        nc.sync.dma_start(coef[:], a.rearrange("(b p i) -> p b i", b=2, i=PACK))
-        nc.sync.dma_start(table[1][:], tab_words[1].rearrange("p n t -> p (n t)").bitcast(I32))
-
-        neg_coef = keep.tile([P, 2, PACK], F32, name="neg_coef")
-        nc.scalar.activation(neg_coef[:], coef[:], COPY, scale=-1.0)
+        nc.sync.dma_start(table[0][:], tab_words[0].rearrange("p n t -> p (n t)").bitcast(I32))
+        nc.sync.dma_start(list2[:], offs2)
 
         scale_rows = keep.tile([P, S], U8, name="scale_rows", align_bytes=64)
         nc.vector.tensor_copy(scale_rows[:], scale_win[:].indirect(list1[:]))
-        for k in range(2):
+
+        def place_plane(k):
             for q in range(4):
-                engine = nc.gpsimd if k == 1 and q > 0 else nc.scalar
-                row = 16 * k + 4 * q
-                engine.dma_start(
+                row = 96 + 16 * k + 4 * q
+                nc.sync.dma_start(
                     planes[k][32 * q : 32 * q + 4, :].bitcast(I32), scale_rows[row : row + 4, :].bitcast(I32)
                 )
-        w1_raw.append(reuse.tile([P, 2, H], U8, name="w1_raw1", tag="slot_a", align_bytes=64))
-        nc.sync.dma_start(w1_raw[1][:].bitcast(I32), w1_rows[:, :, H : 2 * H].bitcast(I32))
+
+        place_plane(0)
+        table.append(reuse.tile([P, T], I32, name="table1", tag="slot_a", align_bytes=64))
+        nc.sync.dma_start(table[1][:], tab_words[1].rearrange("p n t -> p (n t)").bitcast(I32))
+        place_plane(1)
 
         w1_s = keep.tile([P, 2, H], U8, name="w1_s", align_bytes=64)
         nc.vector.tensor_copy(
@@ -93,8 +89,15 @@ def tile_list_granular_waveshaper_kernel(
             return dealt
 
         w1_q = [deal_w1(0)]
-        env = reuse.tile([P, STEPS], F32, name="env", tag="slot_w", align_bytes=64)
-        nc.sync.dma_start(env[:], wgt)
+        env_coef = reuse.tile([P, STEPS + 2 * PACK], F32, name="env_coef", tag="slot_b", align_bytes=64)
+        env = env_coef[:, 0:STEPS]
+        coef = env_coef[:, STEPS:]
+        w1_raw.append(reuse.tile([P, 2, H], U8, name="w1_raw1", tag="slot_w", align_bytes=64))
+        nc.sync.dma_start(w1_raw[1][:].bitcast(I32), w1_rows[:, :, H : 2 * H].bitcast(I32))
+        nc.sync.dma_start(env, wgt)
+        nc.sync.dma_start(coef.rearrange("p (b i) -> p b i", b=2), a.rearrange("(b p i) -> p b i", b=2, i=PACK))
+        neg_coef = keep.tile([P, 2, PACK], F32, name="neg_coef")
+        nc.gpsimd.tensor_scalar(neg_coef[:].rearrange("p b i -> p (b i)"), coef, -1.0, 0.0, MULT, ADD)
         picked = [[None, None], [None, None]]
         for k in range(2):
             for s in range(2):
@@ -107,7 +110,7 @@ def tile_list_granular_waveshaper_kernel(
             nc.sync.dma_start(
                 w2_raw[:, b, :], w2[512 * b : 512 * (b + 1), :].rearrange("(p j) n -> p (j n)", j=PACK)
             )
-        gains = reuse.tile([P, PACK], F32, name="gains", tag="slot_a", align_bytes=64)
+        gains = reuse.tile([P, PACK], F32, name="gains", tag="slot_w", align_bytes=64)
         nc.sync.dma_start(gains[:], gain.rearrange("(p t) -> p t", t=PACK))
 
         def first_product(acc, b, i, s, k):
@@ -122,21 +125,12 @@ def tile_list_granular_waveshaper_kernel(
                 stop=(k == 1),
             )
 
-        opened = {}
-        for s in range(2):
-            for i in range(PACK):
-                opened[i, s] = psum.tile([P, BANK], F32, name="acc", tag="bank")
-                first_product(opened[i, s], 0, i, s, 0)
-
         def make_h(b, i):
             rows = reuse.tile([P, S], F32, name="h%d%d" % (b, i), tag="h%d%d" % (b, i), align_bytes=64)
             for s in range(2):
-                if b == 0:
-                    acc = opened[i, s]
-                else:
-                    acc = psum.tile([P, BANK], F32, name="acc", tag="bank")
-                    first_product(acc, b, i, s, 0)
-                first_product(acc, b, i, s, 1)
+                acc = psum.tile([P, BANK], F32, name="acc", tag="bank")
+                for k in range(2):
+                    first_product(acc, b, i, s, k)
                 nc.scalar.activation(rows[:, BANK * s : BANK * (s + 1)], acc[:], COPY)
             return rows
 

@@ -20,8 +20,14 @@ SQUARE = mybir.ActivationFunctionType.Square
 
 P = 128
 PACK = 4
+PASS = P * PACK
 BANK = 512
+PER_COLUMN = 16
 HALF = STEPS // 2
+SCALE_ROW0 = 96
+PAIR = 2
+AHEAD = 2
+FACTORS_ON_VECTOR = 3
 
 
 def tile_list_granular_waveshaper_kernel(
@@ -34,13 +40,14 @@ def tile_list_granular_waveshaper_kernel(
         ring = ctx.enter_context(tc.tile_pool(name="ring", bufs=4))
         psum = ctx.enter_context(tc.psum_pool(name="psum", bufs=8))
 
-        list1 = keep.tile([P, S // 16], U16, name="list1")
-        list2 = keep.tile([P, STEPS // 16], U16, name="list2")
+        list1 = keep.tile([P, S // PER_COLUMN], U16, name="list1")
+        list2 = keep.tile([P, STEPS // PER_COLUMN], U16, name="list2")
         scale_win = reuse.tile([P, T], U8, name="scale_win", tag="slot_a", align_bytes=64)
         w1s_raw = reuse.tile([P, 2, H], U8, name="w1s_raw", tag="slot_b", align_bytes=64)
         planes = [keep.tile([P, S], U8, name="plane%d" % k, align_bytes=64) for k in range(2)]
+
         nc.gpsimd.memset(w1s_raw[:].rearrange("p a c -> p (a c)").bitcast(I32), 0)
-        nc.vector.memset(scale_win[0:96, :].bitcast(I32), 0)
+        nc.vector.memset(scale_win[0:SCALE_ROW0, :].bitcast(I32), 0)
         for k in range(2):
             nc.gpsimd.memset(planes[k][:].bitcast(I32), 0)
 
@@ -49,12 +56,14 @@ def tile_list_granular_waveshaper_kernel(
         table = [reuse.tile([P, T], I32, name="table0", tag="slot_t0", align_bytes=64)]
 
         nc.sync.dma_start(list1[:], offs)
-        nc.sync.dma_start(scale_win[96:P, :].bitcast(I32), tab_scales.rearrange("a q t -> (a q) t").bitcast(I32))
+        nc.sync.dma_start(
+            scale_win[SCALE_ROW0:P, :].bitcast(I32), tab_scales.rearrange("a q t -> (a q) t").bitcast(I32)
+        )
         nc.sync.dma_start(w1_raw[0][:].bitcast(I32), w1_rows[:, :, 0:H].bitcast(I32))
-        for q in range(4):
+        for quad in range(4):
             nc.sync.dma_start(
-                w1s_raw[32 * q : 32 * q + 4, :, :].bitcast(I32),
-                w1_scales[:, 4 * q : 4 * q + 4, :].rearrange("a r c -> r a c").bitcast(I32),
+                w1s_raw[32 * quad : 32 * quad + 4, :, :].bitcast(I32),
+                w1_scales[:, 4 * quad : 4 * quad + 4, :].rearrange("a r c -> r a c").bitcast(I32),
             )
         nc.sync.dma_start(table[0][:], tab_words[0].rearrange("p n t -> p (n t)").bitcast(I32))
         nc.sync.dma_start(list2[:], offs2)
@@ -63,10 +72,10 @@ def tile_list_granular_waveshaper_kernel(
         nc.vector.tensor_copy(scale_rows[:], scale_win[:].indirect(list1[:]))
 
         def place_plane(k):
-            for q in range(4):
-                row = 96 + 16 * k + 4 * q
+            for quad in range(4):
+                row = SCALE_ROW0 + 16 * k + 4 * quad
                 nc.sync.dma_start(
-                    planes[k][32 * q : 32 * q + 4, :].bitcast(I32), scale_rows[row : row + 4, :].bitcast(I32)
+                    planes[k][32 * quad : 32 * quad + 4, :].bitcast(I32), scale_rows[row : row + 4, :].bitcast(I32)
                 )
 
         place_plane(0)
@@ -76,15 +85,15 @@ def tile_list_granular_waveshaper_kernel(
 
         w1_s = keep.tile([P, 2, H], U8, name="w1_s", align_bytes=64)
         nc.vector.tensor_copy(
-            w1_s[:].rearrange("p a (b i m) -> p (a b) i m", b=2, i=PACK),
-            w1s_raw[:].rearrange("p a (b m i) -> p (a b) i m", b=2, i=PACK),
+            w1_s[:].rearrange("p a (b i j) -> p (a b) i j", b=2, i=PACK),
+            w1s_raw[:].rearrange("p a (b j i) -> p (a b) i j", b=2, i=PACK),
         )
 
         def deal_w1(b):
             dealt = keep.tile([P, 2, H], U8, name="w1_q%d" % b, align_bytes=64)
             nc.vector.tensor_copy(
-                dealt[:].bitcast(U16).rearrange("p a (i m) -> p a i m", i=PACK),
-                w1_raw[b][:].bitcast(U16).rearrange("p a (m i) -> p a i m", i=PACK),
+                dealt[:].bitcast(U16).rearrange("p a (i j) -> p a i j", i=PACK),
+                w1_raw[b][:].bitcast(U16).rearrange("p a (j i) -> p a i j", i=PACK),
             )
             return dealt
 
@@ -98,58 +107,58 @@ def tile_list_granular_waveshaper_kernel(
         nc.sync.dma_start(coef.rearrange("p (b i) -> p b i", b=2), a.rearrange("(b p i) -> p b i", b=2, i=PACK))
         neg_coef = keep.tile([P, 2, PACK], F32, name="neg_coef")
         nc.gpsimd.tensor_scalar(neg_coef[:].rearrange("p b i -> p (b i)"), coef, -1.0, 0.0, MULT, ADD)
+
         picked = [[None, None], [None, None]]
         for k in range(2):
             for s in range(2):
-                g = keep.tile([P, BANK], U32, name="picked%d%d" % (k, s), align_bytes=64)
-                nc.vector.tensor_copy(g[:], table[k][:].bitcast(U32).indirect(list1[:, 32 * s : 32 * (s + 1)]))
-                picked[k][s] = g
+                entries = list1[:, s * BANK // PER_COLUMN : (s + 1) * BANK // PER_COLUMN]
+                words = keep.tile([P, BANK], U32, name="picked%d%d" % (k, s), align_bytes=64)
+                nc.vector.tensor_copy(words[:], table[k][:].bitcast(U32).indirect(entries))
+                picked[k][s] = words
         w1_q.append(deal_w1(1))
+
         w2_raw = reuse.tile([P, 2, PACK * N], F32, name="w2_raw", tag="slot_t0", align_bytes=64)
         for b in range(2):
             nc.sync.dma_start(
-                w2_raw[:, b, :], w2[512 * b : 512 * (b + 1), :].rearrange("(p j) n -> p (j n)", j=PACK)
+                w2_raw[:, b, :], w2[PASS * b : PASS * (b + 1), :].rearrange("(p i) n -> p (i n)", i=PACK)
             )
         gains = reuse.tile([P, PACK], F32, name="gains", tag="slot_w", align_bytes=64)
         nc.sync.dma_start(gains[:], gain.rearrange("(p t) -> p t", t=PACK))
 
-        def first_product(acc, b, i, s, k):
-            c0 = 512 * b + P * i
-            nc.tensor.matmul_mx(
-                out=acc[:],
-                lhsT=w1_q[b][:, k, 2 * P * i : 2 * P * (i + 1)].bitcast(FP4X4),
-                lhsT_scale=w1_s[:, k, c0 : c0 + P],
-                rhs=picked[k][s][:].bitcast(FP8X4),
-                rhs_scale=planes[k][:, BANK * s : BANK * (s + 1)],
-                start=(k == 0),
-                stop=(k == 1),
-            )
-
         def make_h(b, i):
             rows = reuse.tile([P, S], F32, name="h%d%d" % (b, i), tag="h%d%d" % (b, i), align_bytes=64)
+            column = PASS * b + P * i
             for s in range(2):
                 acc = psum.tile([P, BANK], F32, name="acc", tag="bank")
                 for k in range(2):
-                    first_product(acc, b, i, s, k)
+                    nc.tensor.matmul_mx(
+                        out=acc[:],
+                        lhsT=w1_q[b][:, k, 2 * P * i : 2 * P * (i + 1)].bitcast(FP4X4),
+                        lhsT_scale=w1_s[:, k, column : column + P],
+                        rhs=picked[k][s][:].bitcast(FP8X4),
+                        rhs_scale=planes[k][:, BANK * s : BANK * (s + 1)],
+                        start=(k == 0),
+                        stop=(k == 1),
+                    )
                 nc.scalar.activation(rows[:, BANK * s : BANK * (s + 1)], acc[:], COPY)
-            return rows
+            h[b].append(rows)
 
-        def chunk_tiles(b, m0, width):
+        def new_run(b, m0, width):
             x = keep.tile([P, PACK, width], F32, name="x%d_%d" % (b, m0), align_bytes=64)
             u = keep.tile([P, PACK, width], F32, name="u%d_%d" % (b, m0), align_bytes=64)
             return b, m0, width, x, u
 
-        def pick(chunk, i):
-            b, m0, width, x, u = chunk
+        def pick(run, i):
+            b, m0, width, x, u = run
             nc.vector.tensor_tensor(
                 x[:, i, :],
-                h[b][i][:].indirect(list2[:, m0 // 16 : (m0 + width) // 16]),
+                h[b][i][:].indirect(list2[:, m0 // PER_COLUMN : (m0 + width) // PER_COLUMN]),
                 env[:, m0 : m0 + width],
                 MULT,
             )
 
-        def factor(chunk, first, count, on_vector):
-            b, m0, width, x, u = chunk
+        def factor(run, first, count, on_vector):
+            b, m0, width, x, u = run
             sq = ring.tile([P, count, width], F32, name="sq", tag="sq")
             nc.scalar.activation(sq[:], x[:, first : first + count, :], SQUARE)
             for i in range(first, first + count):
@@ -160,16 +169,16 @@ def tile_list_granular_waveshaper_kernel(
                         u[:, i, :], sq[:, i - first, :], COPY, bias=1.0, scale=neg_coef[:, b, i : i + 1]
                     )
 
-        def shape(chunk):
-            b, m0, width, x, u = chunk
+        def shape(run):
+            b, m0, width, x, u = run
             z = keep.tile([P, width, PACK], BF16, name="z%d_%d" % (b, m0), align_bytes=64)
             nc.vector.tensor_tensor(
-                z[:].rearrange("p (c e) i -> p c i e", e=2),
-                x[:].rearrange("p i (c e) -> p c i e", e=2),
-                u[:].rearrange("p i (c e) -> p c i e", e=2),
+                z[:].rearrange("p (c e) i -> p c i e", e=PAIR),
+                x[:].rearrange("p i (c e) -> p c i e", e=PAIR),
+                u[:].rearrange("p i (c e) -> p c i e", e=PAIR),
                 MULT,
             )
-            return z
+            return z[:].rearrange("p m i -> p (m i)")
 
         def quantise(name, grouped, width):
             codes = keep.tile([P, width], U32, name=name + "_q", align_bytes=64)
@@ -177,25 +186,34 @@ def tile_list_granular_waveshaper_kernel(
             nc.vector.quantize_mx(codes[:].bitcast(FP8X4), scales[:], grouped)
             return codes, scales
 
-        def round_w2(b, pair):
-            ts = slice(2 * pair, 2 * pair + 2)
-            nc.scalar.activation(
-                w2_bf[b][:, ts].rearrange("p t m j -> p m j t"),
-                w2_raw[:, b, :].rearrange("p (j m t) -> p m j t", j=PACK, t=PACK)[:, :, :, ts],
-                COPY,
-            )
+        def round_copy(dst, src, on_vector):
+            if on_vector:
+                nc.vector.tensor_copy(dst, src)
+            else:
+                nc.scalar.activation(dst, src, COPY)
+
+        def round_w2(b, tag, second_on_vector):
+            grouped = reuse.tile([P, PACK, P, PACK], BF16, name="w2_bf%d" % b, tag=tag, align_bytes=64)
+            for first in range(0, PACK, PAIR):
+                ts = slice(first, first + PAIR)
+                round_copy(
+                    grouped[:, ts].rearrange("p t j i -> p j i t"),
+                    w2_raw[:, b, :].rearrange("p (i j t) -> p j i t", i=PACK, t=PACK)[:, :, :, ts],
+                    second_on_vector and first > 0,
+                )
+            return grouped[:].rearrange("p t j i -> p (t j i)")
 
         y_scales = keep.tile([P, STEPS], U8, name="y_scales", align_bytes=64)
         y_rows = out_0.rearrange("(p t) m -> p t m", t=PACK)
         y_words = out_1[0].rearrange("p m t -> p (m t)").bitcast(I32)
 
-        def mix(s, z1, share):
+        def mix(s, z_late, share):
             m0 = HALF * s
             y = keep.tile([P, PACK, HALF], F32, name="y%d" % s, align_bytes=64)
             for t in range(PACK):
                 acc = psum.tile([P, HALF], F32, name="mix", tag="bank")
                 for b in range(2):
-                    z_q, z_s = (z0, z1)[b]
+                    z_q, z_s = (z_early, z_late)[b]
                     cols = slice(m0, m0 + HALF) if b == 0 else slice(0, HALF)
                     nc.tensor.matmul_mx(
                         out=acc[:],
@@ -213,10 +231,12 @@ def tile_list_granular_waveshaper_kernel(
             nc.sync.dma_start(y_rows[:, :, m0 : m0 + HALF], y[:])
             return y
 
-        def round_y(s, y):
+        def round_y(s, y, on_vector):
             y_bf = keep.tile([P, HALF, PACK], BF16, name="y_bf%d" % s, align_bytes=64)
-            nc.vector.tensor_copy(
-                y_bf[:].rearrange("p (c e) t -> p c t e", e=2), y[:].rearrange("p t (c e) -> p c t e", e=2)
+            round_copy(
+                y_bf[:].rearrange("p (c e) t -> p c t e", e=PAIR),
+                y[:].rearrange("p t (c e) -> p c t e", e=PAIR),
+                on_vector,
             )
             return y_bf
 
@@ -228,60 +248,48 @@ def tile_list_granular_waveshaper_kernel(
             )
             nc.sync.dma_start(y_words[:, m0 : m0 + HALF], y_q[:].bitcast(I32))
 
-        flat = "p m i -> p (m i)"
         h = [[], []]
-        w2_bf = []
-        c0 = chunk_tiles(0, 0, STEPS)
-        c1 = [chunk_tiles(1, HALF * s, HALF) for s in range(2)]
-        h[0].append(make_h(0, 0))
-        pick(c0, 0)
-        h[0].append(make_h(0, 1))
-        pick(c0, 1)
-        h[0].append(make_h(0, 2))
-        factor(c0, 0, 1, True)
-        pick(c0, 2)
-        h[0].append(make_h(0, 3))
-        factor(c0, 1, 1, True)
-        pick(c0, 3)
-        h[1].append(make_h(1, 0))
-        factor(c0, 2, 1, True)
-        pick(c1[0], 0)
-        h[1].append(make_h(1, 1))
-        factor(c0, 3, 1, True)
-        pick(c1[0], 1)
-        h[1].append(make_h(1, 2))
-        pick(c1[1], 0)
-        zb0 = shape(c0)
-        h[1].append(make_h(1, 3))
-        pick(c1[0], 2)
-        z0 = quantise("z0", zb0[:].rearrange(flat), STEPS)
-        w2_bf.append(reuse.tile([P, PACK, P, PACK], BF16, name="w2_bf0", tag="h02", align_bytes=64))
-        round_w2(0, 0)
-        round_w2(0, 1)
-        pick(c1[0], 3)
-        factor(c1[0], 0, 2, False)
-        factor(c1[0], 2, 2, False)
-        pick(c1[1], 1)
-        w2_q = [quantise("w2_0", w2_bf[0][:].rearrange("p t m j -> p (t m j)"), N)]
-        w2_bf.append(reuse.tile([P, PACK, P, PACK], BF16, name="w2_bf1", tag="h03", align_bytes=64))
-        round_w2(1, 0)
-        round_w2(1, 1)
-        pick(c1[1], 2)
-        zb1 = shape(c1[0])
-        pick(c1[1], 3)
-        z1 = quantise("z1_0", zb1[:].rearrange(flat), HALF)
-        w2_q.append(quantise("w2_1", w2_bf[1][:].rearrange("p t m j -> p (t m j)"), N))
-        factor(c1[1], 0, 2, False)
-        factor(c1[1], 2, 2, True)
-        y0 = mix(0, z1, False)
-        zb1 = shape(c1[1])
-        yb0 = round_y(0, y0)
-        z1 = quantise("z1_1", zb1[:].rearrange(flat), HALF)
-        planes_out(0, yb0)
-        y1 = mix(1, z1, True)
-        planes_out(1, round_y(1, y1))
-        for q in range(4):
-            engine = nc.scalar if q % 2 else nc.sync
+        early = new_run(0, 0, STEPS)
+        late = [new_run(1, HALF * s, HALF) for s in range(2)]
+
+        for n in range(PACK + AHEAD):
+            b, i = divmod(n, PACK)
+            make_h(b, i)
+            if n >= AHEAD:
+                factor(early, n - AHEAD, 1, n - AHEAD < FACTORS_ON_VECTOR)
+            pick((early, late[0])[b], i)
+
+        make_h(1, 2)
+        pick(late[1], 0)
+        z_bf = shape(early)
+        make_h(1, 3)
+        pick(late[0], 2)
+        z_early = quantise("z0", z_bf, STEPS)
+        w2_bf = round_w2(0, "h02", False)
+        pick(late[0], 3)
+        factor(late[0], 0, 2, False)
+        factor(late[0], 2, 2, False)
+        pick(late[1], 1)
+        w2_q = [quantise("w2_0", w2_bf, N)]
+        w2_bf = round_w2(1, "h03", True)
+        pick(late[1], 2)
+        z_bf = shape(late[0])
+        pick(late[1], 3)
+        z_first = quantise("z1_0", z_bf, HALF)
+        w2_q.append(quantise("w2_1", w2_bf, N))
+        factor(late[1], 0, 2, False)
+        factor(late[1], 2, 2, True)
+
+        y_first = mix(0, z_first, False)
+        z_bf = shape(late[1])
+        y_first_bf = round_y(0, y_first, False)
+        z_second = quantise("z1_1", z_bf, HALF)
+        planes_out(0, y_first_bf)
+        y_second = mix(1, z_second, True)
+        planes_out(1, round_y(1, y_second, True))
+
+        for quad in range(4):
+            engine = nc.scalar if quad % 2 else nc.sync
             engine.dma_start(
-                out_2[0, 4 * q : 4 * q + 4, :].bitcast(I32), y_scales[32 * q : 32 * q + 4, :].bitcast(I32)
+                out_2[0, 4 * quad : 4 * quad + 4, :].bitcast(I32), y_scales[32 * quad : 32 * quad + 4, :].bitcast(I32)
             )

from contextlib import ExitStack

import concourse.mybir as mybir

K, H, N, T, S, STEPS = 1024, 1024, 512, 4096, 1024, 512
FLOPS = 2 * K * H * S + 2 * H * N * STEPS

F32 = mybir.dt.float32
BF16 = mybir.dt.bfloat16
I32 = mybir.dt.int32
U32 = mybir.dt.uint32
U16 = mybir.dt.uint16
U8 = mybir.dt.uint8
FP8X4 = mybir.dt.float8_e4m3fn_x4
FP4X4 = mybir.dt.float4_e2m1fn_x4
MULT = mybir.AluOpType.mult
ADD = mybir.AluOpType.add
COPY = mybir.ActivationFunctionType.Copy
SQUARE = mybir.ActivationFunctionType.Square

P = 128
PACK = 4
PASS = P * PACK
BANK = 512
PER_COLUMN = 16
HALF = STEPS // 2
SCALE_ROW0 = 96
PAIR = 2
AHEAD = 2
FACTORS_ON_VECTOR = 3


def tile_list_granular_waveshaper_kernel(
    tc, tab_words, tab_scales, offs, w1_words, w1_scales, wgt, offs2, a, w2, gain, out_0, out_1, out_2
):
    nc = tc.nc
    with ExitStack() as ctx:
        keep = ctx.enter_context(tc.tile_pool(name="keep", bufs=1))
        reuse = ctx.enter_context(tc.tile_pool(name="reuse", bufs=1))
        ring = ctx.enter_context(tc.tile_pool(name="ring", bufs=4))
        psum = ctx.enter_context(tc.psum_pool(name="psum", bufs=8))

        list1 = keep.tile([P, S // PER_COLUMN], U16, name="list1")
        list2 = keep.tile([P, STEPS // PER_COLUMN], U16, name="list2")
        scale_win = reuse.tile([P, T], U8, name="scale_win", tag="slot_a", align_bytes=64)
        w1s_raw = reuse.tile([P, 2, H], U8, name="w1s_raw", tag="slot_b", align_bytes=64)
        planes = [keep.tile([P, S], U8, name="plane%d" % k, align_bytes=64) for k in range(2)]

        nc.gpsimd.memset(w1s_raw[:].rearrange("p a c -> p (a c)").bitcast(I32), 0)
        nc.vector.memset(scale_win[0:SCALE_ROW0, :].bitcast(I32), 0)
        for k in range(2):
            nc.gpsimd.memset(planes[k][:].bitcast(I32), 0)

        w1_rows = w1_words.rearrange("a p c -> p a c")
        w1_raw = [reuse.tile([P, 2, H], U8, name="w1_raw0", tag="slot_w", align_bytes=64)]
        table = [reuse.tile([P, T], I32, name="table0", tag="slot_t0", align_bytes=64)]

        nc.sync.dma_start(list1[:], offs)
        nc.sync.dma_start(
            scale_win[SCALE_ROW0:P, :].bitcast(I32), tab_scales.rearrange("a q t -> (a q) t").bitcast(I32)
        )
        nc.sync.dma_start(w1_raw[0][:].bitcast(I32), w1_rows[:, :, 0:H].bitcast(I32))
        for quad in range(4):
            nc.sync.dma_start(
                w1s_raw[32 * quad : 32 * quad + 4, :, :].bitcast(I32),
                w1_scales[:, 4 * quad : 4 * quad + 4, :].rearrange("a r c -> r a c").bitcast(I32),
            )
        nc.sync.dma_start(table[0][:], tab_words[0].rearrange("p n t -> p (n t)").bitcast(I32))
        nc.sync.dma_start(list2[:], offs2)

        scale_rows = keep.tile([P, S], U8, name="scale_rows", align_bytes=64)
        nc.vector.tensor_copy(scale_rows[:], scale_win[:].indirect(list1[:]))

        def place_plane(k):
            for quad in range(4):
                row = SCALE_ROW0 + 16 * k + 4 * quad
                nc.sync.dma_start(
                    planes[k][32 * quad : 32 * quad + 4, :].bitcast(I32), scale_rows[row : row + 4, :].bitcast(I32)
                )

        place_plane(0)
        table.append(reuse.tile([P, T], I32, name="table1", tag="slot_a", align_bytes=64))
        nc.sync.dma_start(table[1][:], tab_words[1].rearrange("p n t -> p (n t)").bitcast(I32))
        place_plane(1)

        w1_s = keep.tile([P, 2, H], U8, name="w1_s", align_bytes=64)
        nc.vector.tensor_copy(
            w1_s[:].rearrange("p a (b i j) -> p (a b) i j", b=2, i=PACK),
            w1s_raw[:].rearrange("p a (b j i) -> p (a b) i j", b=2, i=PACK),
        )

        def deal_w1(b):
            dealt = keep.tile([P, 2, H], U8, name="w1_q%d" % b, align_bytes=64)
            nc.vector.tensor_copy(
                dealt[:].bitcast(U16).rearrange("p a (i j) -> p a i j", i=PACK),
                w1_raw[b][:].bitcast(U16).rearrange("p a (j i) -> p a i j", i=PACK),
            )
            return dealt

        w1_q = [deal_w1(0)]
        env_coef = reuse.tile([P, STEPS + 2 * PACK], F32, name="env_coef", tag="slot_b", align_bytes=64)
        env = env_coef[:, 0:STEPS]
        coef = env_coef[:, STEPS:]
        w1_raw.append(reuse.tile([P, 2, H], U8, name="w1_raw1", tag="slot_w", align_bytes=64))
        nc.sync.dma_start(w1_raw[1][:].bitcast(I32), w1_rows[:, :, H : 2 * H].bitcast(I32))
        nc.sync.dma_start(env, wgt)
        nc.sync.dma_start(coef.rearrange("p (b i) -> p b i", b=2), a.rearrange("(b p i) -> p b i", b=2, i=PACK))
        neg_coef = keep.tile([P, 2, PACK], F32, name="neg_coef")
        nc.gpsimd.tensor_scalar(neg_coef[:].rearrange("p b i -> p (b i)"), coef, -1.0, 0.0, MULT, ADD)

        picked = [[None, None], [None, None]]
        for k in range(2):
            for s in range(2):
                entries = list1[:, s * BANK // PER_COLUMN : (s + 1) * BANK // PER_COLUMN]
                words = keep.tile([P, BANK], U32, name="picked%d%d" % (k, s), align_bytes=64)
                nc.vector.tensor_copy(words[:], table[k][:].bitcast(U32).indirect(entries))
                picked[k][s] = words
        w1_q.append(deal_w1(1))

        w2_raw = reuse.tile([P, 2, PACK * N], F32, name="w2_raw", tag="slot_t0", align_bytes=64)
        for b in range(2):
            nc.sync.dma_start(
                w2_raw[:, b, :], w2[PASS * b : PASS * (b + 1), :].rearrange("(p i) n -> p (i n)", i=PACK)
            )
        gains = reuse.tile([P, PACK], F32, name="gains", tag="slot_w", align_bytes=64)
        nc.sync.dma_start(gains[:], gain.rearrange("(p t) -> p t", t=PACK))

        def make_h(b, i):
            rows = reuse.tile([P, S], F32, name="h%d%d" % (b, i), tag="h%d%d" % (b, i), align_bytes=64)
            column = PASS * b + P * i
            for s in range(2):
                acc = psum.tile([P, BANK], F32, name="acc", tag="bank")
                for k in range(2):
                    nc.tensor.matmul_mx(
                        out=acc[:],
                        lhsT=w1_q[b][:, k, 2 * P * i : 2 * P * (i + 1)].bitcast(FP4X4),
                        lhsT_scale=w1_s[:, k, column : column + P],
                        rhs=picked[k][s][:].bitcast(FP8X4),
                        rhs_scale=planes[k][:, BANK * s : BANK * (s + 1)],
                        start=(k == 0),
                        stop=(k == 1),
                    )
                nc.scalar.activation(rows[:, BANK * s : BANK * (s + 1)], acc[:], COPY)
            h[b].append(rows)

        def new_run(b, m0, width):
            x = keep.tile([P, PACK, width], F32, name="x%d_%d" % (b, m0), align_bytes=64)
            u = keep.tile([P, PACK, width], F32, name="u%d_%d" % (b, m0), align_bytes=64)
            return b, m0, width, x, u

        def pick(run, i):
            b, m0, width, x, u = run
            nc.vector.tensor_tensor(
                x[:, i, :],
                h[b][i][:].indirect(list2[:, m0 // PER_COLUMN : (m0 + width) // PER_COLUMN]),
                env[:, m0 : m0 + width],
                MULT,
            )

        def factor(run, first, count, on_vector):
            b, m0, width, x, u = run
            sq = ring.tile([P, count, width], F32, name="sq", tag="sq")
            nc.scalar.activation(sq[:], x[:, first : first + count, :], SQUARE)
            for i in range(first, first + count):
                if on_vector:
                    nc.vector.tensor_scalar(u[:, i, :], sq[:, i - first, :], neg_coef[:, b, i : i + 1], 1.0, MULT, ADD)
                else:
                    nc.scalar.activation(
                        u[:, i, :], sq[:, i - first, :], COPY, bias=1.0, scale=neg_coef[:, b, i : i + 1]
                    )

        def shape(run):
            b, m0, width, x, u = run
            z = keep.tile([P, width, PACK], BF16, name="z%d_%d" % (b, m0), align_bytes=64)
            nc.vector.tensor_tensor(
                z[:].rearrange("p (c e) i -> p c i e", e=PAIR),
                x[:].rearrange("p i (c e) -> p c i e", e=PAIR),
                u[:].rearrange("p i (c e) -> p c i e", e=PAIR),
                MULT,
            )
            return z[:].rearrange("p m i -> p (m i)")

        def quantise(name, grouped, width):
            codes = keep.tile([P, width], U32, name=name + "_q", align_bytes=64)
            scales = keep.tile([P, width], U8, name=name + "_s", align_bytes=64)
            nc.vector.quantize_mx(codes[:].bitcast(FP8X4), scales[:], grouped)
            return codes, scales

        def round_copy(dst, src, on_vector):
            if on_vector:
                nc.vector.tensor_copy(dst, src)
            else:
                nc.scalar.activation(dst, src, COPY)

        def round_w2(b, tag, second_on_vector):
            grouped = reuse.tile([P, PACK, P, PACK], BF16, name="w2_bf%d" % b, tag=tag, align_bytes=64)
            for first in range(0, PACK, PAIR):
                ts = slice(first, first + PAIR)
                round_copy(
                    grouped[:, ts].rearrange("p t j i -> p j i t"),
                    w2_raw[:, b, :].rearrange("p (i j t) -> p j i t", i=PACK, t=PACK)[:, :, :, ts],
                    second_on_vector and first > 0,
                )
            return grouped[:].rearrange("p t j i -> p (t j i)")

        y_scales = keep.tile([P, STEPS], U8, name="y_scales", align_bytes=64)
        y_rows = out_0.rearrange("(p t) m -> p t m", t=PACK)
        y_words = out_1[0].rearrange("p m t -> p (m t)").bitcast(I32)

        def mix(s, z_late, share):
            m0 = HALF * s
            y = keep.tile([P, PACK, HALF], F32, name="y%d" % s, align_bytes=64)
            for t in range(PACK):
                acc = psum.tile([P, HALF], F32, name="mix", tag="bank")
                for b in range(2):
                    z_q, z_s = (z_early, z_late)[b]
                    cols = slice(m0, m0 + HALF) if b == 0 else slice(0, HALF)
                    nc.tensor.matmul_mx(
                        out=acc[:],
                        lhsT=w2_q[b][0][:, P * t : P * (t + 1)].bitcast(FP8X4),
                        lhsT_scale=w2_q[b][1][:, P * t : P * (t + 1)],
                        rhs=z_q[:, cols].bitcast(FP8X4),
                        rhs_scale=z_s[:, cols],
                        start=(b == 0),
                        stop=(b == 1),
                    )
                if share and t % 2:
                    nc.vector.tensor_scalar(y[:, t, :], acc[:], gains[:, t : t + 1], None, MULT)
                else:
                    nc.scalar.activation(y[:, t, :], acc[:], COPY, scale=gains[:, t : t + 1])
            nc.sync.dma_start(y_rows[:, :, m0 : m0 + HALF], y[:])
            return y

        def round_y(s, y, on_vector):
            y_bf = keep.tile([P, HALF, PACK], BF16, name="y_bf%d" % s, align_bytes=64)
            round_copy(
                y_bf[:].rearrange("p (c e) t -> p c t e", e=PAIR),
                y[:].rearrange("p t (c e) -> p c t e", e=PAIR),
                on_vector,
            )
            return y_bf

        def planes_out(s, y_bf):
            m0 = HALF * s
            y_q = keep.tile([P, HALF], U32, name="y_q%d" % s, align_bytes=64)
            nc.vector.quantize_mx(
                y_q[:].bitcast(FP8X4), y_scales[:, m0 : m0 + HALF], y_bf[:].rearrange("p m t -> p (m t)")
            )
            nc.sync.dma_start(y_words[:, m0 : m0 + HALF], y_q[:].bitcast(I32))

        h = [[], []]
        early = new_run(0, 0, STEPS)
        late = [new_run(1, HALF * s, HALF) for s in range(2)]

        for n in range(PACK + AHEAD):
            b, i = divmod(n, PACK)
            make_h(b, i)
            if n >= AHEAD:
                factor(early, n - AHEAD, 1, n - AHEAD < FACTORS_ON_VECTOR)
            pick((early, late[0])[b], i)

        make_h(1, 2)
        pick(late[1], 0)
        z_bf = shape(early)
        make_h(1, 3)
        pick(late[0], 2)
        z_early = quantise("z0", z_bf, STEPS)
        w2_bf = round_w2(0, "h02", False)
        pick(late[0], 3)
        factor(late[0], 0, 2, False)
        factor(late[0], 2, 2, False)
        pick(late[1], 1)
        w2_q = [quantise("w2_0", w2_bf, N)]
        w2_bf = round_w2(1, "h03", True)
        pick(late[1], 2)
        z_bf = shape(late[0])
        pick(late[1], 3)
        z_first = quantise("z1_0", z_bf, HALF)
        w2_q.append(quantise("w2_1", w2_bf, N))
        factor(late[1], 0, 2, False)
        factor(late[1], 2, 2, True)

        y_first = mix(0, z_first, False)
        z_bf = shape(late[1])
        y_first_bf = round_y(0, y_first, False)
        z_second = quantise("z1_1", z_bf, HALF)
        planes_out(0, y_first_bf)
        y_second = mix(1, z_second, True)
        planes_out(1, round_y(1, y_second, True))

        for quad in range(4):
            engine = nc.scalar if quad % 2 else nc.sync
            engine.dma_start(
                out_2[0, 4 * quad : 4 * quad + 4, :].bitcast(I32), y_scales[32 * quad : 32 * quad + 4, :].bitcast(I32)
            )
